import numpy as np, ml_dtypes
CORES = [25,29,65,69,153,157,193,197]
N = 8
import mx_ref
BF = ml_dtypes.bfloat16
def gentries(a):
    return np.ascontiguousarray(a.reshape(8, 16, -1).transpose(0, 2, 1)).reshape(8, -1)
def gtable(e):
    e = np.asarray(e); return np.ascontiguousarray(e.reshape(8, -1, 16).transpose(0, 2, 1)).reshape(128, -1).astype(np.int32)
def gcols(t, e):
    v = np.concatenate([t.reshape(8, 16, -1, 4), np.zeros((8, 16, 1, 4), BF)], axis=2)
    return np.ascontiguousarray(np.stack([v[g][:, e[g]] for g in range(8)])).reshape(128, -1)
def tile(rs):
    return np.stack(rs, axis=2).reshape(128, -1).astype(BF)
def pick(q, e):
    c = np.concatenate([q[0].reshape(128, -1, 4), np.zeros((128, 1, 4), np.uint8)], axis=1); s = np.concatenate([q[1], np.ones((16, 1), np.uint8)], axis=1)
    return (np.ascontiguousarray(c[:, e].reshape(128, -1)), np.ascontiguousarray(s[:, e]))
def join(*qs):
    return (np.concatenate([q[0] for q in qs], axis=1), np.concatenate([q[1] for q in qs], axis=1))
def put(q, e, v):
    c, s = q[0].reshape(128, -1, 4).copy(), q[1].copy(); c[:, e] = v[0].reshape(128, -1, 4); s[:, e] = v[1]
    return (c.reshape(128, -1), s)
def pk(c, s):
    return (np.ascontiguousarray(c), mx_ref.live(s))
def emit(q):
    return q[0], q[1]
def packed(v, rng):
    q = [mx_ref.quantize(np.ascontiguousarray(v[r])) for r in range(N)]
    return np.stack([a for a, b in q]), np.stack([mx_ref.plane(b, rng) for a, b in q])
def values_of_codes():
    e, c = np.zeros((128, 128, 4), np.float32), np.zeros((128, 2, 4), np.uint8)
    e[np.arange(128), np.arange(128), 0] = 1
    c[:127, :, 0] = np.arange(256).reshape(2, 128).T[:127]
    return mx_ref.matmul(mx_ref.quantize(e.reshape(128, 512).astype(BF)), (c.reshape(128, 8), np.full((16, 2), 127, np.uint8))).T.reshape(-1).astype(np.float64)
CODE_VALUE, SCALE_VALUE = values_of_codes(), 2.0 ** (np.arange(256) - 127.0)
def decode(q):
    return (CODE_VALUE[q[0]].reshape(16, 8, -1, 4) * SCALE_VALUE[q[1]][:, None, :, None] + 0.0).reshape(128, -1).astype(np.float32)
def f(rng, *shape):
    return mx_ref.flush((rng.standard_normal(shape, dtype=np.float32) * np.exp2(rng.integers(-2, 3, shape[:-1] + (1,)))).astype(BF))
def wide(rng, *shape, cols=0):
    v = rng.standard_normal(shape, dtype=np.float32) * np.exp2(rng.integers(-12, 13, shape)).astype(np.float32)
    if cols: v *= np.repeat(np.exp2(rng.integers(-cols, cols + 1, shape[:-2] + (1, shape[-1] // 4))) * (rng.random(shape[:-2] + (1, shape[-1] // 4)) > 0.0625), 4, axis=-1).astype(np.float32)
    return mx_ref.flush(v.astype(BF))
C, H, R = 320, 128, 3
def numbers_of(rng):
    return {"x": np.array(f(rng, N, 128, 4 * C)), "u": np.array(f(rng, N, 128, 512)), "v": np.array(f(rng, N, 128, 512))}
def orders(rng):
    return np.argsort(rng.random((N, 8, C)), axis=2)
def bonds(e):
    return np.stack([gtable(e[r]) for r in range(N)])
def layers(rng, still=()):
    w = np.array(f(rng, N, 128, 2048)).reshape(N, 8, 16, 4, 8, 16, 4)
    for i in still:
        w[:, :, i] = 0
        w[:, :, :, :, :, i] = 0
    return w
def weights(rng, w):
    c, p = packed(np.ascontiguousarray(w).reshape(N, 128, 2048), rng)
    return {"wc": c, "ws": p}
def chosen(rng, n):
    k, a = np.arange(8 * n), np.zeros((8, C), bool)
    a[k % 8, k // 4] = True
    return a[:, rng.permutation(C)]
def crowd(rng):
    n, o = H + 1, rng.permutation(C)
    full, half, none, rest = o[:48], o[48:48 + n], o[48 + n:48 + 2 * n], o[48 + 2 * n:]
    a, e = np.zeros((8, C), bool), np.zeros((8, C), np.int64)
    a[:, full] = True
    for j in range(n): a[(j + 1 + rng.permutation(7)[:4]) % 8, half[j]] = True
    for g in range(8):
        b = np.concatenate([half[g::8], rng.permutation(np.delete(half, np.arange(g, n, 8)))])
        e[g, none] = rng.permutation(half)
        e[g, b[:48]] = rng.permutation(full)
        e[g, np.concatenate([b[48:], full])] = rng.permutation(none)
        e[g, rest] = rng.permutation(rest)
    return a, e
def faint():
    k = 2.0 ** -np.arange(4.0, 28.0)
    t = np.zeros((128, 24, 4), np.float32)
    t[0, :, 0] = 1.96875
    t[7, :, 0] = k
    once = decode(mx_ref.quantize(t.reshape(128, 96).astype(BF)))
    again = decode(mx_ref.quantize(once.astype(BF)))
    i = int(np.argmax((once[7, ::4] > 0) & (again[7, ::4] == 0)))
    assert once[7, 4 * i] == k[i] and again[7, 4 * i] == 0
    return k[i]
def plant(d, s):
    x = d["x"].reshape(N, 8, 16, C, 4)
    x[:, :, 0] = 0
    x[:, :, 0, :, 0] = s.astype(np.float32).astype(BF)
    u = d["u"].reshape(N, 128, 128, 4)
    u[:, :, ::16] = 0
    for h in range(0, 128, 16): u[:, h, h, 0] = 1
def setup_inputs(rng):
    return {**numbers_of(rng), "m": bonds(orders(rng)), **weights(rng, layers(rng))}
def setup_inputs_slots(rng):
    d = numbers_of(rng)
    e, s, c, h = orders(rng), np.zeros((N, 8, C)), int(rng.integers(4)), H // 2
    for r in range(N):
        k = (r + c) % 4
        if k == 0:
            a = chosen(rng, H)
            for g in rng.permutation(8)[:4]: a[g, rng.choice(np.flatnonzero(a[g]))] = False
        elif k == 1: a = chosen(rng, H + 1)
        elif k == 2:
            o = rng.permutation(C)
            a = np.zeros((8, C), bool)
            a[:, o[:h]] = True
            for g in range(8):
                e[r, g, o[h:2 * h]] = rng.permutation(o[:h])
                e[r, g, o[2 * h:3 * h]] = rng.permutation(o[h:2 * h])
                e[r, g, o[:h]] = rng.permutation(o[2 * h:3 * h])
                e[r, g, o[3 * h:]] = rng.permutation(o[3 * h:])
        else: a, e[r] = crowd(rng)
        s[r] = np.where(a, 1.0, -1.0 * rng.integers(0, 2, (8, C)))
    plant(d, s)
    x = d["x"].reshape(N, 8, 16, C, 4)
    x[:, :, 8:11] = 0
    x[:, :, 8, :, 0] = 1
    u = d["u"].reshape(N, 128, 128, 4)
    for i in range(0, 128, 16): u[:, i + 10, i, 0] = 1
    w, o = layers(rng, (0, 8, 9, 10)), rng.permutation(8)
    w[:, :, 8, 0, :, 9, 0] = 4
    for r in range(N):
        for j in range(8): w[r, :, 9, 0, o[(2 * r + j) % 8], 10, 0] = 512 if j < 4 else -512
    return {**d, "m": bonds(e), **weights(rng, w)}
def setup_inputs_near(rng):
    d = numbers_of(rng)
    x = d["x"].astype(np.float32).reshape(N, 8, 16, C, 4)
    x[:, :, :2] = 0
    x[:, :, 8:] = 0
    c = rng.choice([-1.0, 1.0], (N, 8, C))
    a = rng.choice([-1.0, 0.0, 1.0, 1.0], (3, N, 8, C))
    x[:, :, 0, :, 0] = c
    x[:, :, 1, :, 0] = -c
    x[:, :, 8, :, 0] = a[0] * 2.0 ** -30
    x[:, :, 9, :, 0] = a[1] * 2.0 ** -23
    x[:, :, 10, :, 0] = a[2] * 1.125 * 2.0 ** -30
    x[:, :, 11, :, 0] = a[2] * -1.0 * 2.0 ** -30
    u = d["u"].reshape(N, 128, 128, 4)
    u[:, :, ::16] = 0
    o = rng.permutation(N) % 3
    for r in range(N):
        if o[r] == 0:
            for g in rng.permutation(8)[:4]: x[r, g, 8, rng.integers(C), 0] = 2.0 ** 30 * rng.choice([-1.0, 1.0])
        for h in range(0, 128, 16):
            if o[r] == 0: u[r, h + 8, h, 0] = 2.0 ** -30
            elif o[r] == 1:
                u[r, h + 10, h, 0] = 1.125 * 2.0 ** -30
                u[r, h + 11, h, 0] = 1.25 * 2.0 ** -30
            else:
                for i in (0, 1, 9): u[r, h + i, h, 0] = 1
    return {"x": x.reshape(N, 128, 4 * C).astype(BF), "u": d["u"], "v": d["v"], "m": bonds(orders(rng)), **weights(rng, layers(rng, (0, 1, 8, 9, 10, 11, 12, 13, 14, 15)))}
def setup_inputs_late(rng):
    d = numbers_of(rng)
    k = np.argsort(rng.random((N, 8, C)), axis=1)
    known = k < 4 + (rng.permutation(N) % 2)[:, None, None]
    plant(d, np.where(k == 0, 0.0, np.where(known, 1.0, -1.0)))
    x = d["x"].reshape(N, 8, 16, C, 4)
    n = (N, 8, 8, C, 4)
    a = (1 + (2 * rng.integers(0, 64, n) + 1) * 2.0 ** -7) * np.exp2(rng.integers(-14, -7, n))
    a[:, :, 0, :, 0] = 1.96875
    x[:, :, 8:] = (a * (2.0 * rng.integers(0, 2, n) - 1.0)).astype(np.float32).astype(BF)
    x[:, :, 15, :, 0] = np.where(k == 0, faint(), 0.0).astype(np.float32).astype(BF)
    u = d["u"].reshape(N, 128, 128, 4)
    for h in range(0, 128, 16): u[:, h + 15, h, 0] = 1
    return {**d, "m": bonds(orders(rng)), **weights(rng, layers(rng))}
def setup_inputs_ends(rng):
    d = numbers_of(rng)
    x, e, c, i = np.zeros((N, 8, 16, C, 4)), orders(rng), int(rng.integers(4)), np.arange(128)
    u, v = d["u"].reshape(N, 128, 128, 4), d["v"]
    u[:, :, ::16] = 0
    w = np.zeros((N, 128, 4, 128, 4), np.float32)
    for r in range(N):
        k = (r + c) % 4
        a = (0.75 + 0.25 * rng.random((8, 16, C, 4))) * 2.0 ** 30
        for j in range(4): w[r, i, j, i, j] = 2.0 ** -30
        if k == 0:
            x[r] = a * rng.choice([-1.0, 1.0], C)[:, None]
            s = np.where(rng.permutation(8) < 5, 1.0, -1.0)
            for g in range(8): u[r, :, 16 * g] = s[g] * 2.0 ** 30
            e[r] = np.arange(C)[::-1]
            v[r] = (2.0 ** 30 * rng.choice([-1.0, 1.0], (128, 512))).astype(np.float32).astype(BF)
            n = i[i % 16 < 8]
            for j in range(4): w[r, n, j, n, j] = -1
        elif k == 1:
            x[r] = (1 + 0.25 * rng.integers(0, 4, (8, 16, C, 4))) * 2.0 ** -30
            x[r, :, :8] *= 2.0
            u[r, :, ::16] = 2.0 ** -30
            e[r] = np.arange(C)
            v[r] = (2.0 ** -30 * rng.choice([-1.0, 1.0], (128, 512))).astype(np.float32).astype(BF)
        elif k == 2:
            x[r] = -a
            u[r, :, ::16] = 2.0 ** 30
        else:
            x[r] = a * np.where(chosen(rng, H), 1.0, -1.0)[:, None, :, None]
            for g in range(8): u[r, 16 * g:16 * g + 16, 16 * g] = 2.0 ** 30
            e[r] = rng.permutation(C)
    return {"x": x.astype(np.float32).reshape(N, 128, 4 * C).astype(BF), "u": d["u"], "v": v, "m": bonds(e), **weights(rng, w.astype(BF))}
def setup_inputs_spread(rng):
    d = setup_inputs(rng)
    d["x"] = wide(rng, N, 128, 4 * C, cols=6)
    return d
def check_inputs(d):
    b = []
    for k in ("x", "u", "v"):
        a = np.abs(d[k].astype(np.float32))
        if not (np.isfinite(a).all() and ((a == 0) | (a >= 2.0 ** -30) & (a <= 2.0 ** 30)).all()): b.append("a value of " + k)
    none, least, most = [emit(mx_ref.quantize(np.full((128, 16), k, np.float32).astype(BF)))[1][0, 0] for k in (0.0, 2.0 ** -30, 2.0 ** 30)]
    for r in range(N):
        if (np.sort(gentries(d["m"][r]), axis=1) != np.arange(C)).any(): b.append("m: a list that is no permutation")
        if ((d["wc"][r] == 0x7F) | (d["wc"][r] == 0xFF)).any(): b.append("wc: a code that is no number")
        s = mx_ref.live(d["ws"][r])
        if ((s != none) & ((s < least) | (s > most))).any(): b.append("ws: a scale out of range")
    return b
def waves(s, to):
    w = np.where(s > 0, 1, 4)
    for t in (2, 3):
        licensed = np.count_nonzero(w < 4, axis=0) >= 5
        w = np.where((w == 4) & licensed[to], t, w)
    return w
def reference(x, u, v, m, wc, ws):
    qu = [mx_ref.quantize(u[r]) for r in range(N)]
    lay = [pk(wc[r], ws[r]) for r in range(N)]
    now = [x[r] for r in range(N)]
    lists = np.stack([gentries(m[r]) for r in range(N)])
    for t in range(R):
        to = np.roll(lists, -t, axis=1)
        own, wave, sent = [], [], []
        for r in range(N):
            q = mx_ref.quantize(now[r])
            own.append(decode(q).astype(BF))
            wave.append(waves(mx_ref.matmul(qu[r], q)[::16], to[r]))
            o = np.argsort(np.where(wave[r] < 4, 3 - wave[r], 3), axis=1, kind="stable")[:, :H]
            e = np.where(np.take_along_axis(wave[r], o, axis=1) < 4, o, -1)
            sent.append(mx_ref.quantize(gcols(own[r], e)))
        for r in range(N):
            guests = decode(sent[(r - 1) % N]).astype(BF)
            k = np.argsort(np.argsort(wave[r] < 4, axis=1, kind="stable"), axis=1)
            e = np.where(wave[r] == 1, np.arange(C), np.where(wave[r] < 4, to[r], C + k % H))
            z = gcols(np.concatenate([own[r], guests], axis=1), e)
            q = mx_ref.quantize(z)
            made = tile([mx_ref.matmul(pick(lay[r], np.arange(128 * b, 128 * b + 128)), q) * np.float32(0.03125) + z[:, b::4].astype(np.float32) for b in range(4)])
            now[r] = gcols(made, np.argsort(to[r], axis=1))
    y, wv = np.zeros((N, 128, C), np.float32), np.zeros((N, 8, C), np.float32)
    oc, osc = np.zeros((N, 128, 4 * C), np.uint8), np.zeros((N, 16, C), np.uint8)
    for r in range(N):
        q = mx_ref.quantize(now[r])
        y[r] = mx_ref.matmul(mx_ref.quantize(v[r]), q)
        wv[r] = wave[r]
        oc[r], osc[r] = emit(q)
    return {"y": y, "wv": wv, "oc": oc, "osc": osc}

from concourse.bass import DstId, RemoteDMATransfer
from concourse.mybir import dt, AluOpType, ActivationFunctionType

C, H, R = 320, 128, 3
UP = 512
CODES, PLANE = "float8_e4m3fn_x4", "uint8"
SCRATCH = {
    "P": ("psum", [128, 4096], "float32"),
    "x0": ("sbuf", [128, 4 * C], "bfloat16"), "xt": ("sbuf", [128, 4 * C], "bfloat16"),
    "ut": ("sbuf", [128, 512], "bfloat16"), "vb": ("sbuf", [128, 512], "bfloat16"),
    "qu": ("sbuf", [128, 128], CODES), "su": ("sbuf", [128, 128], PLANE),
    "qu2": ("sbuf", [128, 128], CODES), "su2": ("sbuf", [128, 128], PLANE),
    "qv": ("sbuf", [128, 128], CODES), "sv": ("sbuf", [128, 128], PLANE),
    "qw": ("sbuf", [128, 512], CODES), "sw": ("sbuf", [128, 512], PLANE),
    "qx": ("sbuf", [128, C], CODES), "sx": ("sbuf", [128, C], PLANE),
    "qz": ("sbuf", [128, C], CODES), "sz": ("sbuf", [128, C], PLANE),
    "mi": ("sbuf", [128, 60], "int32"), "m20": ("sbuf", [128, 60], "uint16"),
    "ones": ("sbuf", [128, 516], "bfloat16"), "mones": ("sbuf", [128, 512], "bfloat16"),
    "cn": ("sbuf", [128, 520], "bfloat16"), "ed": ("sbuf", [128, 516], "bfloat16"),
    "ka": ("sbuf", [128, 512], "bfloat16"), "kan": ("sbuf", [128, 512], "bfloat16"),
    "kp": ("sbuf", [128, 512], "bfloat16"), "kr": ("sbuf", [128, 512], "bfloat16"),
    "kb": ("sbuf", [128, 512], "bfloat16"), "kbn": ("sbuf", [128, 512], "bfloat16"), "kc": ("sbuf", [128, 512], "bfloat16"),
    "qn": ("sbuf", [128, 512], CODES), "sn": ("sbuf", [128, 512], PLANE),
    "qe": ("sbuf", [128, 512], CODES), "se": ("sbuf", [128, 512], PLANE),
    "qk": ("sbuf", [128, 640], CODES), "sk": ("sbuf", [128, 640], PLANE),
    "uo32": ("sbuf", [128, 8], "int32"), "uoff": ("sbuf", [128, 8], "uint16"),
    "pc": ("sbuf", [128, 4], "int32"), "pd": ("sbuf", [128, 4], "int32"), "cols": ("sbuf", [128, 16], "float32"),
    "i80": ("sbuf", [128, 80], "float32"), "i320": ("sbuf", [128, C], "float32"), "iv": ("sbuf", [128, C], "float32"),
    "mb": ("sbuf", [128, C], "float32"), "mt": ("sbuf", [128, 80], "float32"),
    "d1": ("sbuf", [128, 512], "bfloat16"), "d2": ("sbuf", [128, 512], "bfloat16"), "d3": ("sbuf", [128, 512], "bfloat16"),
    "qd1": ("sbuf", [128, 128], CODES), "sd1": ("sbuf", [128, 128], PLANE),
    "qd2": ("sbuf", [128, 128], CODES), "sd2": ("sbuf", [128, 128], PLANE),
    "qd3": ("sbuf", [128, 128], CODES), "sd3": ("sbuf", [128, 128], PLANE),
    "l1": ("sbuf", [128, C], "bfloat16"), "l2": ("sbuf", [128, C], "bfloat16"),
    "fw": ("sbuf", [128, 4 * (C + H)], "bfloat16"), "gg": ("sbuf", [128, 4 * C + 16], "bfloat16"),
    "zt": ("sbuf", [128, 4 * C], "bfloat16"), "z32": ("sbuf", [128, 4 * C], "bfloat16"), "vt": ("sbuf", [128, 4 * C], "float32"),
    "wn": ("sbuf", [128, UP + C], "float32"), "off20": ("sbuf", [128, 20], "uint16"),
    "m128": ("sbuf", [128, 128], "float32"), "h64": ("sbuf", [128, 64], "float32"), "h32": ("sbuf", [128, 32], "float32"),
    "kint": ("sbuf", [128, 80], "int32"), "kand": ("sbuf", [128, 80], "int32"), "zo": ("sbuf", [128, 80], "uint16"),
    "t320": ("sbuf", [128, C], "float32"), "t160": ("sbuf", [128, 160], "float32"), "invw": ("sbuf", [128, C], "float32"),
    "wv1": ("sbuf", [128, C], "float32"), "ysb": ("sbuf", [128, C], "float32"),
}
SMALL = ("zero", "bf80", "tf80", "i0", "i4", "f1w", "f3w", "sc1", "p1", "sc2", "p2", "p12", "sc3", "p3", "p3i", "p12n", "ps", "pm",
         "a40", "a20", "sck", "ngk", "gk", "ba", "bb", "bc", "bd", "zi", "t80")
SCRATCH["small"] = ("sbuf", [128, 80 * len(SMALL)], "float32")
for _t in range(R):
    SCRATCH["qf%d" % _t] = ("sbuf", [128, C], CODES)
    SCRATCH["sf%d" % _t] = ("sbuf", [128, C], PLANE)
    SCRATCH["lc%d" % _t] = ("sbuf", [128, C], CODES)
    SCRATCH["ls%d" % _t] = ("sbuf", [128, C], PLANE)
    SCRATCH["lo%d" % _t] = ("sbuf", [128, 32], "uint16")
    SCRATCH["ll%d" % _t] = ("sbuf", [128, 32], "uint16")
    SCRATCH["mi4%d" % _t] = ("sbuf", [128, 80], "float32")
    SCRATCH["inv%d" % _t] = ("sbuf", [128, 80], "uint16")

SEMAPHORES = ["kT", "kV", "kS", "kG", "dx", "du", "dv", "dm", "dw", "dr", "do", "dy", "snd"]
SEMAPHORES += ["%s%d" % (a, t) for a in ("ca", "cb", "cp", "cl") for t in range(R)]

HALF = C // 2


def mask_of(engines):
    return sum(1 << e for e in engines)


def road(T, topo, r):
    src, dst = T.cores[r], T.cores[(r + 1) % len(T.cores)]
    if topo.may_write(src, dst):
        return dst, [dst, dst, dst]
    own = [c for c in topo.cores_of(src) if c not in T.cores and topo.may_write(c, dst)]
    near = [c for c in own if topo.die(c) == topo.die(src)]
    far = [c for c in own if topo.die(c) != topo.die(src)]
    return dst, [near[0], near[1], far[0]]


def spread(topo, a, b):
    e = topo.engines(a, b)
    return e[:len(e) // 2], e[len(e) // 2:], e


def hand_on(g, core, T, topo):
    for r in range(len(T.cores)):
        dst, hops = road(T, topo, r)
        if core not in hops:
            continue
        src = T.cores[r]
        rid, pid = topo.addr(dst, core)
        out = topo.engines(core, dst)
        lo, hi, every = spread(topo, src, core)
        sent = 0
        for t in range(R):
            for k, part, eng, view in (("ca", 0, lo, T["lc%d" % t][:, 0:HALF].bitcast(dt.uint8)),
                                       ("cb", 1, hi, T["lc%d" % t][:, HALF:C].bitcast(dt.uint8)),
                                       ("cp", 2, every, T["ls%d" % t][:, 0:C]),
                                       ("cl", 2, every, T["ll%d" % t][:, :])):
                if core == hops[part]:
                    g.wait_ge(T.sem[k + str(t)], len(eng))
                    g.remote_dma(view, view, T.sem[k + str(t)], T.sem.snd, pid, rid, mask_of(out))
                    sent += len(out)
        g.wait_ge(T.sem.snd, sent)


def rank_program(g, core, T, topo):
    rank = T.rank_of(core)
    if rank is None:
        hand_on(g, core, T, topo)
        return
    A = AluOpType
    F = ActivationFunctionType
    V, S, TE = g.vector, g.scalar, g.tensor
    queue = {"T": TE, "V": V, "S": S, "G": g, "Y": g.sync}
    count = {"T": 0, "V": 0, "S": 0, "G": 0}
    total = {}
    known = {q: {} for q in queue}
    snaps = {}
    writer, readers = {}, {}

    def wait(q, event):
        name, val = event
        if known[q].get(name, 0) >= val:
            return
        queue[q].wait_ge(T.sem[name], val)
        for n, v in snaps.get(event, {}).items():
            known[q][n] = max(known[q].get(n, 0), v)
        known[q][name] = val

    def before(q, r, w):
        own = "k" + q
        need = {}
        for k in tuple(r) + tuple(w):
            for e in writer.get(k, ()):
                if not (q == "T" and e[0] == own):
                    need[e[0]] = max(need.get(e[0], 0), e[1])
        for k in w:
            for e in readers.get(k, ()):
                if e[0] != own:
                    need[e[0]] = max(need.get(e[0], 0), e[1])
        for n in sorted(need):
            wait(q, (n, need[n]))

    def after(q, event, r, w):
        snaps[event] = dict(known[q])
        for k in r:
            readers.setdefault(k, []).append(event)
        for k in w:
            writer[k] = [event]
            readers[k] = []

    def op(q, call, r=(), w=()):
        before(q, r, w)
        count[q] += 1
        call().then_inc(T.sem["k" + q], 1)
        after(q, ("k" + q, count[q]), r, w)

    def dmas(q, pairs, sem, r=(), w=()):
        before(q, r, w)
        for o, i in pairs:
            queue[q].dma_start(o, i).then_inc(T.sem[sem], 16)
            total[sem] = total.get(sem, 0) + 16
        after(q, (sem, total[sem]), r, w)

    def bank(k, n):
        return T.P[:, 512 * k:512 * k + n]

    def tt(o, a, b, f, r, w):
        op("V", lambda: V.tensor_tensor(o, a, b, f), r, w)

    def ts(o, a, s1, s2, f1, f2, r, w):
        if f2 is None:
            op("V", lambda: V.tensor_scalar(o, a, s1, None, f1), r, w)
        else:
            op("V", lambda: V.tensor_scalar(o, a, s1, s2, f1, f2), r, w)

    def copy(o, a, r, w):
        op("V", lambda: V.tensor_copy(o, a), r, w)

    def fill(o, c, w):
        op("V", lambda: V.memset(o, c), (), w)

    def act(o, a, f, r, w, **kw):
        op("S", lambda: S.activation(o, a, f, **kw), r, w)

    def quant(q, s, t, r, w):
        op("V", lambda: V.quantize_mx(q, s, t), r, w)

    def mm(k, n, st, mv, r, start=True, stop=True):
        op("T", lambda: TE.matmul_mx(bank(k, n), st[0], st[1], mv[0], mv[1], start, stop), r, ("B%d" % k,))

    def part(n, a, b):
        j = 80 * SMALL.index(n)
        return T.small[:, j + a:j + b]

    W = {n: part(n, 0, 80) for n in SMALL}

    def scan(o, k, init, r=()):
        op("V", lambda: V.tensor_tensor_scan(W[o], bank(k, 80), W["zero"], init, A.add, A.add), tuple(r) + ("zero", "B%d" % k), (o,))

    def add(o, a, b, f, r=()):
        va, vb = (bank(z, 80) if z in range(8) else W[z] for z in (a, b))
        ka, kb = ("B%d" % z if z in range(8) else z for z in (a, b))
        tt(W[o], va, vb, f, (ka, kb) + tuple(r), (o,))

    tcol, bcol, gcol = (T.cols[:, j:j + 1] for j in range(3))

    dmas("S", [(T.x0[:, :], T.x[:, :])], "dx", (), ("X0",))
    dmas("Y", [(T.ut[:, :], T.u[:, :])], "du", (), ("ut",))
    pairs = [(T.mi[:, 0:20], T.m[:, :])]
    for t in range(1, R):
        pairs.append((T.mi[0:128 - 16 * t, 20 * t:20 * t + 20], T.m[16 * t:128, :]))
        pairs.append((T.mi[128 - 16 * t:128, 20 * t:20 * t + 20], T.m[0:16 * t, :]))
    dmas("Y", pairs, "dm", (), ("mi",))
    dmas("Y", [(T.qw[:, 0:512].bitcast(dt.uint8), T.wc[:, :]), (T.sw[:, 0:512], T.ws[:, :])], "dw", (), ("qw",))
    dmas("Y", [(T.vb[:, :], T.v[:, :])], "dv", (), ("vb",))

    fill(T.ones[:, :], 1.0, ("ones",))
    fill(T.mones[:, :], -1.0, ("mones",))
    op("G", lambda: g.iota(T.uo32[:, :], [[16, 8]], 0, 0), (), ("uo32",))
    op("G", lambda: g.iota(T.pc[:, :], [[0, 4]], 0, 1), (), ("pc",))
    op("G", lambda: g.iota(T.i80[:, :], [[1, 80]], 0, 0, allow_small_or_imprecise_dtypes=True), (), ("i80",))
    op("G", lambda: g.affine_select(T.ed[:, :], T.ones[:, :], [[-1, 516]], A.is_equal, 0.0, 3, 4), ("ones",), ("ed",))
    group = [[-16, 8], [0, 64]]
    leg = [[-4, 32], [0, 4], [4, 4]]
    op("G", lambda: g.affine_select(T.ka[:, :], T.ones[:, 0:512], group, A.is_equal, 0.0, 0, 1), ("ones",), ("ka",))
    op("G", lambda: g.affine_select(T.kp[:, :], T.mones[:, :], leg, A.is_gt, 0.0, 0, 1), ("mones",), ("kp",))
    op("G", lambda: g.affine_select(T.kr[:, :], T.kp[:, :], leg, A.not_equal, 1024.0, 0, 1), ("kp",), ("kr",))
    op("G", lambda: g.affine_select(T.kb[:, :], T.kr[:, :], group, A.is_equal, 0.0, 0, 1), ("kr",), ("kb",))
    op("G", lambda: g.affine_select(T.kc[:, :], T.ka[:, :], leg, A.is_equal, 0.0, 0, 1), ("ka",), ("kc",))

    fill(W["zero"], 0.0, ("zero",))
    copy(T.uoff[:, :], T.uo32[:, :], ("uo32",), ("uoff",))
    op("V", lambda: V.tensor_scalar(T.pd[:, 0:1], T.pc[:, 0:1], 3, None, A.bitwise_and), ("pc",), ("pd0",))
    op("V", lambda: V.tensor_scalar(T.pd[:, 1:2], T.pc[:, 0:1], 2, 3, A.arith_shift_right, A.bitwise_and), ("pc",), ("pd1",))
    copy(T.cols[:, 0:2], T.pd[:, 0:2], ("pd0", "pd1"), ("cols",))
    ts(gcol, tcol, float(4 * C), None, A.add, None, ("cols",), ("gcol",))
    fill(T.cn[:, :], 0.0, ("cn",))
    fill(T.cn[:, 3:520:4], 1.0, ("cn",))
    for d in ("d1", "d2", "d3"):
        fill(T[d][:, C:512], 0.0, (d + "pad",))
    fill(T.gg[:, 4 * C:4 * C + 16], 0.0, ("ggpad",))
    act(W["bf80"], T.i80[:, :], F.Identity, ("i80", "cols"), ("bf80",), scale=0.0, bias=bcol)
    act(W["tf80"], T.i80[:, :], F.Identity, ("i80", "cols"), ("tf80",), scale=0.0, bias=tcol)
    act(W["i0"], T.i80[:, :], F.Identity, ("i80", "cols"), ("i0",), scale=4.0, bias=bcol)
    quant(T.qu[:, :], T.su[:, :], T.ut[:, :], ("ut",), ("qu",))
    copy(T.qu2[:, 0:128].bitcast(dt.uint32), T.qu[:, 0:128].bitcast(dt.uint32).indirect(T.uoff[:, 0:8]), ("qu", "uoff"), ("qu2",))
    act(T.su2[:, 0:128], T.su[:, 0:128].indirect(T.uoff[:, 0:8]), F.Copy, ("qu", "uoff"), ("su2",))
    act(W["i4"], W["i0"], F.Identity, ("i0", "cols"), ("i4",), scale=4.0, bias=tcol)
    for b in range(4):
        act(T.iv[:, b:C:4], T.i80[:, :], F.Copy, ("i80",), ("iv%d" % b,), bias=80.0 * b)
    for b in range(4):
        act(T.i320[:, b:C:4], T.i80[:, :], F.Copy, ("i80",), ("ix%d" % b,), scale=4.0, bias=float(b))
    act(T.kan[:, :], T.ka[:, :], F.Copy, ("ka",), ("kan",), scale=-1.0)
    for b in range(4):
        quant(T.qn[:, 128 * b:128 * b + 128], T.sn[:, 128 * b:128 * b + 128], T.cn[:, 3 - b:515 - b], ("cn",), ("qn%d" % b,))
    for b in range(4):
        quant(T.qe[:, 128 * b:128 * b + 128], T.se[:, 128 * b:128 * b + 128], T.ed[:, 3 - b:515 - b], ("ed",), ("qe%d" % b,))
    copy(T.m20[:, :], T.mi[:, :], ("mi",), ("m20",))
    mbk, mtk, ivk, ixk = (tuple(n + str(b) for b in range(4)) for n in ("mb", "mt", "iv", "ix"))

    place = ("ka", "kan", "kb", "kbn", "kc")

    def const(n):
        j = 128 * place.index(n)
        quant(T.qk[:, j:j + 128], T.sk[:, j:j + 128], T[n][:, :], (n,), ("qk" + n,))

    def K(n):
        j = 128 * place.index(n)
        return (T.qk[:, j:j + 128], T.sk[:, j:j + 128])

    def piece(q, s, b):
        return (T[q][:, 128 * b:128 * b + 128], T[s][:, 128 * b:128 * b + 128])

    dst, hops = road(T, topo, rank)
    _, came = road(T, topo, (rank - 1) % len(T.cores))
    prev = T.cores[(rank - 1) % len(T.cores)]
    lo, hi, every = spread(topo, core, hops[0])
    sent = [0]
    if came[0] == core:
        arrive = spread(topo, prev, core)
    else:
        arrive = [topo.engines(c, core) for c in came]
    for t in range(R):
        for k, e in (("ca", 0), ("cb", 1), ("cp", 2), ("cl", 2)):
            writer[k + str(t)] = [(k + str(t), len(arrive[e]))]

    def send(o, i, sem, to, engines):
        rid, pid = topo.addr(to, core)
        g.remote_dma(o, i, T.sem[sem], T.sem.snd, pid, rid, mask_of(engines))
        sent[0] += len(engines)

    def send_f(t):
        before("G", ("qf%d" % t,), ())
        trs = []
        for hop, eng, a, b, s in ((hops[0], lo, 0, HALF, "ca"), (hops[1], hi, HALF, C, "cb")):
            rid, pid = topo.addr(hop, core)
            trs.append(RemoteDMATransfer(dst_ids=[DstId(rid=rid, pnc=pid)], dma_engine_mask=mask_of(eng), remote_sem=T.sem[s + str(t)],
                                         src=T["qf%d" % t][:, a:b].bitcast(dt.uint8), dst=T["lc%d" % t][:, a:b].bitcast(dt.uint8)))
            sent[0] += len(eng)
        g.remote_dma_fused(trs, local_sem=T.sem.snd)
        send(T["ls%d" % t][:, 0:C], T["sf%d" % t][:, 0:C], "cp%d" % t, hops[2], every)

    qx = (T.qx[:, 0:C], T.sx[:, 0:C])
    qd = {n: (T["q" + n][:, :], T["s" + n][:, :]) for n in ("d1", "d2", "d3")}

    def unpack(b, k):
        mm(k, C, piece("qe", "se", b), qx, ("qe%d" % b, "qx"))

    def f_copy(b, k):
        act(T.fw[:, b:4 * C:4], bank(k, C), F.Copy, ("B%d" % k,), ("fw%d" % b,))

    def counted(d, order):
        for b in order:
            mm(b, 128, piece("qn", "sn", b), qd[d], ("qn%d" % b, "q" + d))

    def licensed(l, order):
        for b in order:
            if b % 2 == 0:
                ts(T[l][:, b:C:4], bank(b, 80), 79.5, None, A.is_ge, None, ("B%d" % b,), (l + str(b),))
            else:
                act(T[l][:, b:C:4], bank(b, 80), F.Sign, ("B%d" % b,), (l + str(b),), bias=-72.0)

    def follow(d, l, old, t):
        lk = tuple(l + str(b) for b in range(4))
        tt(T[d][:, 0:C], T[l][:, 0:C].indirect(T.m20[:, 20 * t:20 * t + 20]), T[old][:, 0:C], A.max, lk + ("m20", old), (d,))
        quant(T["q" + d][:, :], T["s" + d][:, :], T[d][:, :], (d, d + "pad"), ("q" + d,))

    def turned(src):
        tt(T.t160[:, :], src[:, 0:C:2], src[:, 1:C:2], A.add, ("t320",), ("t160",))
        tt(W["t80"], T.t160[:, 0:160:2], T.t160[:, 1:160:2], A.add, ("t160",), ("t80",))

    for t in range(R):
        X, xk = (T.x0, ("X0",)) if t == 0 else (T.xt, ("xa", "xb"))
        quant(T.qx[:, :], T.sx[:, :], X[:, :], xk, ("qx",))
        if t == 0:
            for b in range(4):
                ts(T.mb[:, b:C:4], W["bf80"], float(b), None, A.is_equal, None, ("bf80",), ("mb%d" % b,))
        mm(0, C, (T.qu2[:, :], T.su2[:, :]), qx, ("qu2", "su2", "qx"))
        unpack(0, 4)
        unpack(1, 5)
        ts(T.d1[:, 0:C], bank(0, C), 0.0, None, A.is_gt, None, ("B0",), ("d1",))
        quant(T.qd1[:, :], T.sd1[:, :], T.d1[:, :], ("d1", "d1pad"), ("qd1",))
        f_copy(0, 4)
        f_copy(1, 5)
        counted("d1", (0, 1, 2, 3))
        unpack(2, 6)
        unpack(3, 7)
        if t == 0:
            const("ka")
            const("kan")
        fill(T.wn[:, UP:UP + H], float(C), ("wn",))
        licensed("l1", (0, 1, 2, 3))
        f_copy(2, 6)
        f_copy(3, 7)
        follow("d2", "l1", "d1", t)
        counted("d2", (1, 2, 3, 0))
        if t == 0:
            for b in range(4):
                ts(T.mt[:, 20 * b:20 * b + 20], part("tf80", 0, 20), float(b), None, A.is_equal, None, ("tf80",), ("mt%d" % b,))
            act(T.kbn[:, :], T.kb[:, :], F.Copy, ("kb",), ("kbn",), scale=-1.0)
        quant(T["qf%d" % t][:, :], T["sf%d" % t][:, :], T.fw[:, 0:4 * C], ("fw0", "fw1", "fw2", "fw3"), ("qf%d" % t,))
        send_f(t)
        licensed("l2", (1, 2, 3, 0))
        follow("d3", "l2", "d2", t)
        if t == 0:
            const("kb")
            const("kbn")
        for k, n in ((4, "ka"), (5, "kb")):
            mm(k, 128, K(n), qd["d2"], ("qk" + n, "qd2"), True, False)
            mm(k, 128, K(n + "n"), qd["d1"], ("qk" + n + "n", "qd1"), False, True)
        for k, n in ((6, "ka"), (7, "kb")):
            mm(k, 128, K(n), qd["d1"], ("qk" + n, "qd1"))
        for k, n in ((1, "ka"), (2, "kb")):
            mm(k, 128, K(n + "n"), qd["d2"], ("qk" + n + "n", "qd2"), True, False)
            mm(k, 128, K(n), qd["d3"], ("qk" + n, "qd3"), False, True)
        scan("sc2", 4, float(-UP - 1))
        add("p2", "sc2", 5, A.add)
        scan("sc1", 6, part("sc2", 79, 80), ("sc2",))
        add("p1", "sc1", 7, A.add)
        add("p12", "p1", "p2", A.max)
        scan("sc3", 1, float(-UP - 1))
        add("p3", "sc3", 2, A.add)
        ts(W["p12n"], W["p12"], part("sc3", 79, 80), float(UP + 1), A.add, A.add, ("p12", "sc3"), ("p12n",))
        add("p3i", "p3", "i0", A.max)
        add("ps", "p12n", "p3i", A.max)
        tt(W["pm"], W["ps"], T.mt[:, :], A.mult, ("ps",) + mtk, ("pm",))
        tt(part("a40", 0, 40), part("pm", 0, 40), part("pm", 40, 80), A.add, ("pm",), ("a40",))
        tt(part("a20", 0, 20), part("a40", 0, 20), part("a40", 20, 40), A.add, ("a40",), ("a20",))
        copy(T.off20[:, :], part("a20", 0, 20), ("a20",), ("off20",))
        copy(T.wn[:, 0:UP + C].indirect(T.off20[:, 0:20]), T.iv[:, :], ("off20",) + ivk, ("wn",))
        tt(T.m128[:, :], T.wn[:, UP:UP + H], T.mb[:, 0:H], A.mult, ("wn",) + mbk, ("m128",))
        tt(T.h64[:, :], T.m128[:, 0:128:2], T.m128[:, 1:128:2], A.add, ("m128",), ("h64",))
        tt(T.h32[:, :], T.h64[:, 0:64:2], T.h64[:, 1:64:2], A.add, ("h64",), ("h32",))
        ts(T["lo%d" % t][:, :], T.h32[:, :], 4.0, tcol, A.mult, A.add, ("h32", "cols"), ("lo%d" % t,))
        before("G", ("lo%d" % t,), ())
        send(T["ll%d" % t][:, :], T["lo%d" % t][:, :], "cl%d" % t, hops[2], every)
        if t == 0:
            const("kc")
        mm(3, 128, K("kc"), qd["d1"], ("qkkc", "qd1"))
        mm(4, 128, K("kc"), qd["d3"], ("qkkc", "qd3"))
        mm(5, 128, K("ka"), qd["d3"], ("qkka", "qd3"))
        mm(6, 128, K("kb"), qd["d3"], ("qkkb", "qd3"))
        act(W["f1w"], bank(3, 80), F.Copy, ("B3",), ("f1w",))
        act(W["f3w"], bank(4, 80), F.Copy, ("B4",), ("f3w",))
        for b, k in enumerate((7, 0, 1, 2)):
            mm(k, C, piece("qe", "se", b), (T["lc%d" % t][:, :], T["ls%d" % t][:, :]), ("qe%d" % b, "ca%d" % t, "cb%d" % t, "cp%d" % t))
            act(T.gg[:, b:4 * C:4], bank(k, C), F.Copy, ("B%d" % k,), ("gg%d" % b,))
        scan("sck", 5, 0.0)
        add("ngk", "sck", 6, A.add)
        tt(T.kint[:, :], W["i0"], W["ngk"], A.subtract, ("i0", "ngk"), ("kint",))
        op("V", lambda: V.tensor_scalar(T.kand[:, :], T.kint[:, :], H - 1, None, A.bitwise_and), ("kint",), ("kand",))
        ts(W["gk"], T.kand[:, :], 4.0, gcol, A.mult, A.add, ("kand", "gcol"), ("gk",))
        m0 = T.m20[:, 0:20]
        if t == 0:
            tt(T.t320[:, :], T.i320[:, 0:C].indirect(m0), T.mb[:, :], A.mult, ixk + ("m20",) + mbk, ("t320",))
            turned(T.t320)
            ts(T.mi40[:, :], W["t80"], 4.0, tcol, A.mult, A.add, ("t80", "cols"), ("mi40",))
        mi4, mk = T["mi4%d" % t][:, :], "mi4%d" % t
        tt(W["ba"], W["i4"], mi4, A.subtract, ("i4", mk), ("ba",))
        add("bb", "ba", "f1w", A.mult)
        tt(W["bc"], W["bb"], mi4, A.add, ("bb", mk), ("bc",))
        add("bd", "bc", "gk", A.subtract)
        add("zi", "bd", "f3w", A.mult)
        add("t80", "zi", "gk", A.add)
        copy(T.zo[:, :], W["t80"], ("t80",), ("zo",))
        if t == 0:
            copy(T.invw[:, 0:C].indirect(m0), T.i320[:, :], ixk + ("m20",), ("invw",))
            tt(T.t320[:, :], T.invw[:, :], T.mb[:, :], A.mult, ("invw",) + mbk, ("t320",))
            turned(T.t320)
            ts(T.inv0[:, :], W["t80"], 4.0, tcol, A.mult, A.add, ("t80", "cols"), ("inv0",))
            pairs = []
            for s in range(1, R):
                for n in ("mi4", "inv"):
                    a, b = T[n + str(s)], T[n + "0"]
                    pairs.append((a[0:128 - 16 * s, :], b[16 * s:128, :]))
                    pairs.append((a[128 - 16 * s:128, :], b[0:16 * s, :]))
            dmas("Y", pairs, "dr", ("mi40", "inv0"), tuple(n + str(s) for n in ("mi4", "inv") for s in range(1, R)))
            quant(T.qv[:, :], T.sv[:, :], T.vb[:, :], ("vb",), ("qv",))
        if t == R - 1:
            tt(T.t320[:, :], T.d1[:, 0:C], T.d2[:, 0:C], A.add, ("d1", "d2"), ("t320",))
            tt(T.invw[:, :], T.t320[:, :], T.d3[:, 0:C], A.add, ("t320", "d3"), ("invw",))
            ts(T.wv1[:, :], T.invw[:, :], -1.0, 4.0, A.mult, A.add, ("invw",), ("wv1",))
            dmas("Y", [(T.wv[:, :], T.wv1[0:128:16, :])], "do", ("wv1",), ())
        ggk = ("gg0", "gg1", "gg2", "gg3", "ggpad", "cl%d" % t)
        ll = T["ll%d" % t]
        copy(T.fw[:, 4 * C:4 * C + 256], T.gg[:, 0:4 * C + 16].indirect(ll[:, 0:16]), ggk, ("fwg0",))
        act(T.fw[:, 4 * C + 256:4 * C + 512], T.gg[:, 0:4 * C + 16].indirect(ll[:, 16:32]), F.Copy, ggk, ("fwg1",))
        fwk = ("fw0", "fw1", "fw2", "fw3", "fwg0", "fwg1", "zo")
        copy(T.zt[:, 0:640], T.fw[:, :].indirect(T.zo[:, 0:40]), fwk, ("za",))
        act(T.zt[:, 640:1280], T.fw[:, :].indirect(T.zo[:, 40:80]), F.Copy, fwk, ("zb",))
        quant(T.qz[:, :], T.sz[:, :], T.zt[:, :], ("za", "zb"), ("qz",))
        for b in range(4):
            k = 3 + b
            mm(k, C, piece("qw", "sw", b), (T.qz[:, :], T.sz[:, :]), ("qw", "qz"))
            act(T.z32[:, C * b:C * b + C], T.zt[:, b:4 * C:4], F.Copy, ("za", "zb"), ("z32%d" % b,), scale=32.0)
            tt(T.vt[:, b:4 * C:4], bank(k, C), T.z32[:, C * b:C * b + C], A.add, ("B%d" % k, "z32%d" % b), ("vt%d" % b,))
        vk = ("vt0", "vt1", "vt2", "vt3", "inv%d" % t)
        inv = T["inv%d" % t]
        ts(T.xt[:, 0:640], T.vt[:, :].indirect(inv[:, 0:40]), 0.03125, None, A.mult, None, vk, ("xa",))
        act(T.xt[:, 640:1280], T.vt[:, :].indirect(inv[:, 40:80]), F.Copy, vk, ("xb",), scale=0.03125)

    quant(T.qx[:, :], T.sx[:, :], T.xt[:, :], ("xa", "xb"), ("qx",))
    mm(0, C, (T.qv[:, :], T.sv[:, :]), qx, ("qv", "qx"))
    dmas("Y", [(T.oc[:, 0:4 * C], T.qx[:, 0:C].bitcast(dt.uint8))] +
         [(T.osc[4 * k:4 * k + 4, 0:C], T.sx[32 * k:32 * k + 4, 0:C]) for k in range(4)], "do", ("qx",), ())
    act(T.ysb[:, :], bank(0, C), F.Copy, ("B0",), ("ysb",))
    dmas("S", [(T.y[:, :], T.ysb[:, :])], "dy", ("ysb",), ())
    for q in ("T", "V", "S", "G"):
        g.wait_ge(T.sem["k" + q], count[q])
    g.wait_ge(T.sem.snd, sent[0])
    g.wait_ge(T.sem.do, total["do"])
    g.wait_ge(T.sem.dy, total["dy"])
